import numpy as np
import ml_dtypes


def mxq(x, axis, fmt="e4m3"):
    dtype, down = {"e4m3": (ml_dtypes.float8_e4m3fn, 7), "e5m2": (ml_dtypes.float8_e5m2, 14)}[fmt]
    v = np.moveaxis(np.asarray(x, np.float32).astype(ml_dtypes.bfloat16).astype(np.float64), axis, -1)
    blocks = v.reshape(v.shape[:-1] + (-1, 32))
    amax = np.abs(blocks).max(-1, keepdims=True)
    byte = np.maximum(np.where(amax > 0, np.frexp(amax)[1] - 1 + 127, 0) - down, 1)
    scale = np.exp2(byte - 127.0)
    codes = (blocks / scale).astype(np.float32).astype(dtype).astype(np.float64)
    return np.moveaxis((codes * scale).reshape(v.shape), -1, axis)


WIDE = False


def mx_kscale(k):
    if not WIDE:
        return np.ones(k)
    levels = np.array([10, -10, 5, -5, 0])
    if k % 512:
        return np.exp2(np.random.permutation(np.resize(levels, k // 32))).repeat(32)
    a = np.empty((k // 512, 16))
    for p in range(k // 512):
        a[p, :8] = np.random.permutation(np.resize(levels, 8))
        for g in range(8):
            far = levels[np.abs(levels - a[p, g]) >= 10]
            a[p, g + 8] = far[np.random.randint(len(far))]
    return np.exp2(a.ravel()).repeat(32)


def f64(x):
    return np.asarray(x).astype(np.float64)


def striped(idx):
    return np.tile(np.asarray(idx).reshape(-1, 16).T, (8, 1)).astype(np.uint16)


def unstriped(offs):
    return offs[:16].T.reshape(-1).astype(np.int64)


E2M1 = np.array([0.0, 0.5, 1.0, 1.5, 2.0, 3.0, 4.0, 6.0, -0.0, -0.5, -1.0, -1.5, -2.0, -3.0, -4.0, -6.0])


def pack_weight(w, fmt):
    k, n = w.shape
    w = f64(np.asarray(w, np.float32).astype(ml_dtypes.bfloat16)).reshape(k // 32, 32, n)
    amax = np.abs(w).max(1)
    if fmt == "e4m3":
        byte = np.frexp(amax)[1] - 1 + 127 - 7
    else:
        mant, ex = np.frexp(amax / 6.0)
        byte = np.where(mant > 0.5, ex, ex - 1) + 127
    byte = np.clip(np.where(amax > 0, byte, 1), 1, 254)
    scaled = (w * np.exp2(127.0 - byte)[:, None, :]).reshape(k, n).astype(np.float32)
    by_word = np.ascontiguousarray(scaled.reshape(k // 512, 128, 4, n).transpose(0, 1, 3, 2))
    if fmt == "e4m3":
        words = by_word.astype(ml_dtypes.float8_e4m3fn).view(np.uint8)
    else:
        c = by_word.astype(ml_dtypes.float4_e2m1fn).view(np.uint8) & 0xF
        words = (c[..., 0::2] | (c[..., 1::2] << 4)).reshape(k // 512, 128, 2 * n)
    return np.ascontiguousarray(words), np.ascontiguousarray(byte.astype(np.uint8).reshape(k // 512, 16, n))


def unpack_weight(words, scales, fmt):
    g, _, n = scales.shape
    words = np.ascontiguousarray(words).reshape(g, 128, n, -1)
    if fmt == "e4m3":
        vals = words.view(ml_dtypes.float8_e4m3fn).astype(np.float64)
    else:
        nib = np.empty((g, 128, n, 4), np.uint8)
        nib[..., 0::2] = words & 0xF
        nib[..., 1::2] = words >> 4
        vals = E2M1[nib]
    vals = vals * np.repeat(np.exp2(scales.astype(np.float64) - 127.0), 8, axis=1)[..., None]
    return vals.transpose(0, 1, 3, 2).reshape(g * 512, n)


def silu(v):
    return v / (1.0 + np.exp(-v))


def bf(x):
    return np.asarray(x, np.float32).astype(ml_dtypes.bfloat16)


def planes(Y):
    r, m = Y.shape
    b = f64(bf(Y)).reshape(r // 32, 32, m)
    amax = np.abs(b).max(1)
    byte = np.clip(np.where(amax > 0, np.frexp(amax)[1] - 1 + 127 - 7, 1), 1, 254)
    codes = (b * np.exp2(127.0 - byte)[:, None, :]).reshape(r, m).astype(np.float32).astype(ml_dtypes.float8_e4m3fn).view(np.uint8)
    words = codes.reshape(r // 512, 128, 4, m).transpose(0, 1, 3, 2)
    return np.ascontiguousarray(words), np.ascontiguousarray(byte.astype(np.uint8).reshape(r // 512, 16, m))


B, N, T, D, NQ = 1, 512, 2048, 512, 512
DV = 512


def sgn(shape):
    return np.random.uniform(0.5, 2.0, shape) * np.where(np.random.standard_normal(shape) < 0, -1.0, 1.0)


def setup_inputs():
    n = np.random.standard_normal
    idx = np.random.permutation(T)[:B * N]
    s = mx_kscale(D)[:, None]
    u = mx_kscale(N)
    ut = np.ones(T)
    ut[idx] = u
    kp = pack_weight(n((D, T)) / s, "e4m3")
    cp = pack_weight(n((D, T)) / s, "e4m3")
    return {
        "qT": (n((B, D, NQ)) * s * (1.00 / np.sqrt(D))).astype(np.float32),
        "k_words": kp[0],
        "k_scales": kp[1],
        "c_words": cp[0],
        "c_scales": cp[1],
        "vT": (n((DV, T)) / ut).astype(np.float32),
        "rs": (n((B, DV, NQ))).astype(np.float32),
        "us": (sgn((B, N, 1)) * u[:, None]).astype(np.float32),
        "offs": striped(idx),
    }


def reference(qT, k_words, k_scales, c_words, c_scales, vT, rs, us, offs):
    idx = unstriped(offs)
    pick = lambda x, which: x[:, which].reshape(x.shape[0], B, -1).transpose(1, 0, 2)
    k = unpack_weight(k_words, k_scales, "e4m3")
    kg = pick(k, idx)
    c = unpack_weight(c_words, c_scales, "e4m3")
    cg = pick(c, idx)
    qq = mxq(f64(qT), 1, "e4m3")
    a = kg.transpose(0, 2, 1) @ qq
    z = cg.transpose(0, 2, 1) @ qq
    y = silu(a) * z * f64(us)
    wq = mxq(y, 1, "e4m3")
    o = mxq(pick(f64(vT), idx).transpose(0, 2, 1), 1, "e4m3").transpose(0, 2, 1) @ wq
    r_ = o + f64(rs)
    Y = r_[0]
    words, scales = planes(Y)
    return Y, words, scales

from contextlib import ExitStack

import concourse.mybir as mybir
from concourse.masks import make_identity

F32 = mybir.dt.float32
BF16 = mybir.dt.bfloat16
I32 = mybir.dt.int32
U32 = mybir.dt.uint32
U16 = mybir.dt.uint16
U8 = mybir.dt.uint8
FP8X4 = mybir.dt.float8_e4m3fn_x4
ACT = mybir.ActivationFunctionType
ALU = mybir.AluOpType

P = 128
PACK = 4
N = 512
T = 2048
NQ = 512
HALF = NQ // 2
QUADS = 4
C_ROW = 4
WIN_BYTES = 4 * T

FLOPS = 3 * 2 * 512 * 512 * 512


def weave(engine_copy, dst, src):
    engine_copy(
        out=dst.rearrange("p (c i) t -> p c t i", i=PACK),
        in_=src.rearrange("p t (c i) -> p c t i", i=PACK),
    )


def dealt(tile):
    return tile[:].rearrange("p (r s) -> p s r", r=PACK)


def tile_attend_plo_mlpswiglu_topk_kernel(
    tc, qT, k_words, k_scales, c_words, c_scales, vT, rs, us, offs, out_0, out_1, out_2
):
    nc = tc.nc
    with ExitStack() as ctx:
        sb = ctx.enter_context(tc.tile_pool(name="sb", bufs=1))
        shared = ctx.enter_context(tc.tile_pool(name="shared", bufs=1))
        ps = ctx.enter_context(tc.psum_pool(name="ps", bufs=1))

        def bank(n, shape, name):
            return ps.tile(shape, F32, name=name, tag="bank%d" % n)

        offsets = sb.tile([P, N // 16], U16, name="offsets")
        q_raw = sb.tile([P, PACK, NQ], F32, name="q_raw")
        k_win = sb.tile([P, T], U32, name="k_win")
        c_win = sb.tile([P, T], U32, name="c_win")
        ks_win = sb.tile([P, T], U8, name="ks_win")
        cs_win = sb.tile([P, T], U8, name="cs_win")
        us_sb = sb.tile([P, PACK], F32, name="us_sb")
        v_win = [shared.tile([P, T], F32, name="v_win%d" % j, align_bytes=64, offset=j * WIN_BYTES) for j in range(PACK)]
        rs_sb = [sb.tile([P, NQ], F32, name="rs_sb%d" % j) for j in range(PACK)]
        ident = sb.tile([P, P], F32, name="ident")

        nc.vector.memset(ks_win[:].bitcast(I32), 0)
        nc.vector.memset(cs_win[:].bitcast(I32), 0)
        make_identity(nc, ident[:])

        def load_scales(win, scales, row):
            for quad in range(QUADS):
                nc.sync.dma_start(
                    out=win[32 * quad + row : 32 * quad + row + 4, :].bitcast(I32),
                    in_=scales[0, 4 * quad : 4 * quad + 4, :].bitcast(I32),
                )

        def load_words(win, words):
            nc.sync.dma_start(
                out=win[:].bitcast(I32),
                in_=words[0].rearrange("p t r -> p (t r)").bitcast(I32),
            )

        nc.sync.dma_start(out=q_raw[:], in_=qT[0].rearrange("(p t) q -> p t q", t=PACK))
        nc.sync.dma_start(offsets[:], offs)
        load_scales(ks_win, k_scales, 0)
        load_words(k_win, k_words)
        load_scales(cs_win, c_scales, C_ROW)
        nc.sync.dma_start(out=us_sb[:], in_=us[0].rearrange("(p r) o -> p (r o)", r=PACK))
        load_words(c_win, c_words)
        v_rows = vT.rearrange("(p j) t -> j p t", j=PACK)
        rs_rows = rs[0].rearrange("(p j) q -> j p q", j=PACK)
        out_rows = out_0.rearrange("(p j) q -> j p q", j=PACK)
        for j in range(PACK):
            nc.sync.dma_start(out=v_win[j][:], in_=v_rows[j])
        for j in range(PACK):
            nc.sync.dma_start(out=rs_sb[j][:], in_=rs_rows[j])

        q_bf = sb.tile([P, NQ, PACK], BF16, name="q_bf", align_bytes=64)
        q_codes = sb.tile([P, NQ], U32, name="q_codes", align_bytes=64)
        q_plane = sb.tile([P, NQ], U8, name="q_plane", align_bytes=64)
        k_codes = sb.tile([P, N], U32, name="k_codes", align_bytes=64)
        c_codes = sb.tile([P, N], U32, name="c_codes", align_bytes=64)
        k_plane = sb.tile([P, N], U8, name="k_plane", align_bytes=64)
        c_plane = sb.tile([P, N], U8, name="c_plane", align_bytes=64)

        weave(nc.scalar.copy, q_bf[:], q_raw[:])
        nc.vector.tensor_copy(out=dealt(k_plane), in_=ks_win[:].indirect(offsets[:]))
        nc.vector.tensor_copy(out=dealt(k_codes), in_=k_win[:].indirect(offsets[:]))
        nc.vector.quantize_mx(
            out=q_codes[:].bitcast(FP8X4), scales=q_plane[:], in_=q_bf[:].rearrange("p q t -> p (q t)")
        )
        nc.vector.tensor_copy(out=dealt(c_plane), in_=cs_win[:].indirect(offsets[:]))
        nc.vector.tensor_copy(out=dealt(c_codes), in_=c_win[:].indirect(offsets[:]))

        gate = sb.tile([P, PACK, NQ], F32, name="gate")
        y_rows = sb.tile([P, PACK, NQ], BF16, name="y_rows", tag="y_rows", align_bytes=64)
        for r in range(PACK):
            cols = slice(P * r, P * (r + 1))
            a_ps = bank(r, [P, NQ], "a_ps%d" % r)
            nc.tensor.matmul_mx(
                out=a_ps[:], lhsT=k_codes[:, cols].bitcast(FP8X4), lhsT_scale=k_plane[:, cols],
                rhs=q_codes[:].bitcast(FP8X4), rhs_scale=q_plane[:], start=True, stop=True,
            )
            nc.scalar.activation(out=gate[:, r, :], in_=a_ps[:], func=ACT.Silu)
        for r in range(PACK):
            cols = slice(P * r, P * (r + 1))
            z_ps = bank(PACK + r, [P, NQ], "z_ps%d" % r)
            nc.tensor.matmul_mx(
                out=z_ps[:], lhsT=c_codes[:, cols].bitcast(FP8X4), lhsT_scale=c_plane[C_ROW:P, cols],
                rhs=q_codes[:].bitcast(FP8X4), rhs_scale=q_plane[:], start=True, stop=True,
            )
            nc.vector.scalar_tensor_tensor(
                out=y_rows[:, r, :], in0=z_ps[:], scalar=us_sb[:, r : r + 1], in1=gate[:, r, :],
                op0=ALU.mult, op1=ALU.mult,
            )

        y_bf = sb.tile([P, NQ, PACK], BF16, name="y_bf", tag="y_bf", align_bytes=64)
        y_codes = sb.tile([P, NQ], U32, name="y_codes", align_bytes=64)
        y_plane = sb.tile([P, NQ], U8, name="y_plane", align_bytes=64)

        v_codes = {}
        v_plane = [sb.tile([P, P], U8, name="v_plane%d" % j, align_bytes=64) for j in range(PACK)]
        v_bf = [
            shared.tile([P, P, PACK], BF16, name="v_bf%d" % j, align_bytes=64, offset=(j + 1) * WIN_BYTES)
            for j in range(PACK - 1)
        ]
        v_bf.append(sb.tile([P, P, PACK], BF16, name="v_bf_last", align_bytes=64))

        def gather_and_turn(j, on_vector):
            picked = sb.tile([P, N], BF16, name="v_picked%d" % j)
            if on_vector > 0:
                nc.vector.tensor_copy(
                    out=picked[:, :on_vector], in_=v_win[j][:].indirect(offsets[:, : on_vector // 16])
                )
            if on_vector < N:
                nc.scalar.activation(
                    out=picked[:, on_vector:], in_=v_win[j][:].indirect(offsets[:, on_vector // 16 :]), func=ACT.Copy
                )
            pairs = picked[:].bitcast(F32)
            turned = bank(j % 2, [P, 2, P], "turned%d" % j)
            for u in range(2):
                nc.tensor.transpose(turned[:, u, :], pairs[:, u : N // 2 : 2], ident[:])
            nc.scalar.copy(out=v_bf[j][:].bitcast(F32), in_=turned[:].rearrange("p u e -> p e u"))

        def quantize_v(j):
            tag = "y_rows" if j == 0 else "v_codes%d" % j
            v_codes[j] = sb.tile([P, P], U32, name="v_codes%d" % j, tag=tag, align_bytes=64)
            nc.vector.quantize_mx(
                out=v_codes[j][:].bitcast(FP8X4), scales=v_plane[j][:],
                in_=v_bf[j][:].rearrange("p e t -> p (e t)"),
            )

        def second_layer(j, cols, n, name):
            o_ps = bank(n, [P, cols.stop - cols.start], name)
            nc.tensor.matmul_mx(
                out=o_ps[:], lhsT=v_codes[j][:].bitcast(FP8X4), lhsT_scale=v_plane[j][:],
                rhs=y_codes[:, cols].bitcast(FP8X4), rhs_scale=y_plane[:, cols], start=True, stop=True,
            )
            return o_ps

        res = shared.tile([P, PACK, NQ], F32, name="res", align_bytes=64, offset=3 * WIN_BYTES + 1024)

        def add_residual(j, cols, o_ps):
            nc.vector.tensor_tensor(out=res[:, j, cols], in0=o_ps[:], in1=rs_sb[j][:, cols], op=ALU.add)

        whole = slice(0, NQ)
        halves = [slice(0, HALF), slice(HALF, NQ)]
        last = PACK - 1

        gather_and_turn(0, 0)
        weave(nc.vector.tensor_copy, y_bf[:], y_rows[:])
        nc.vector.quantize_mx(
            out=y_codes[:].bitcast(FP8X4), scales=y_plane[:], in_=y_bf[:].rearrange("p q t -> p (q t)")
        )
        gather_and_turn(1, 0)
        gather_and_turn(2, 0)
        quantize_v(0)
        quantize_v(1)
        o_banks = [second_layer(j, whole, PACK + j, "o_ps%d" % j) for j in range(2)]
        gather_and_turn(last, 320)
        quantize_v(2)
        o_banks.append(second_layer(2, whole, PACK + 2, "o_ps2"))
        quantize_v(last)
        for j in range(last - 1):
            add_residual(j, whole, o_banks[j])
            nc.sync.dma_start(out=out_rows[j], in_=res[:, j, :])
        add_residual(last - 1, whole, o_banks[last - 1])
        nc.sync.dma_start(out=out_rows[last - 1], in_=res[:, last - 1, :])
        for h in range(2):
            o_ps = second_layer(last, halves[h], 2 + h, "o_last%d" % h)
            add_residual(last, halves[h], o_ps)
        nc.sync.dma_start(out=out_rows[last], in_=res[:, last, :])

        res_bf = [sb.tile([P, HALF, PACK], BF16, name="res_bf%d" % h, align_bytes=64) for h in range(2)]
        out_codes = sb.tile([P, NQ], U32, name="out_codes", align_bytes=64)
        out_plane = sb.tile([P, NQ], U8, name="out_plane", align_bytes=64)
        weave(nc.scalar.copy, res_bf[0][:], res[:, :, halves[0]])
        weave(nc.vector.tensor_copy, res_bf[1][:], res[:, :, halves[1]])
        word_rows = out_1[0].rearrange("p q u -> p (q u)").bitcast(I32)
        for h in (1, 0):
            nc.vector.quantize_mx(
                out=out_codes[:, halves[h]].bitcast(FP8X4), scales=out_plane[:, halves[h]],
                in_=res_bf[h][:].rearrange("p q t -> p (q t)"),
            )
            nc.sync.dma_start(out=word_rows[:, halves[h]], in_=out_codes[:, halves[h]].bitcast(I32))
        for quad in range(QUADS):
            queue = nc.scalar if quad % 2 == 0 else nc.sync
            queue.dma_start(
                out=out_2[0, 4 * quad : 4 * quad + 4, :].bitcast(I32),
                in_=out_plane[32 * quad : 32 * quad + 4, :].bitcast(I32),
            )
